import numpy as np, ml_dtypes
CORES = [66,74,82,90,194,202,210,218]
N = 8
import mx_ref
BF = ml_dtypes.bfloat16
def f(rng, *shape):
    return mx_ref.flush((rng.standard_normal(shape, dtype=np.float32) * np.exp2(rng.integers(-2, 3, shape[:-1] + (1,)))).astype(BF))
def wide(rng, *shape, cols=0):
    v = rng.standard_normal(shape, dtype=np.float32) * np.exp2(rng.integers(-12, 13, shape)).astype(np.float32)
    if cols: v *= np.repeat(np.exp2(rng.integers(-cols, cols + 1, shape[:-2] + (1, shape[-1] // 4))) * (rng.random(shape[:-2] + (1, shape[-1] // 4)) > 0.0625), 4, axis=-1).astype(np.float32)
    return mx_ref.flush(v.astype(BF))
def cols(t, e):
    v = np.concatenate([t.reshape(128, -1, 4), np.zeros((128, 1, 4), BF)], axis=1)
    return np.ascontiguousarray(v[:, e]).reshape(128, -1)
def tile(rs):
    return np.stack(rs, axis=2).reshape(128, -1).astype(BF)
def cut(t, i, w=512):
    return t[:, w * i:w * i + w]
def decode(q):
    o = []
    for b in range(4):
        e = np.zeros((128, 128, 4), np.float32); e[np.arange(128), np.arange(128), b] = 1
        o.append(mx_ref.matmul(mx_ref.quantize(e.reshape(128, 512).astype(BF)), q))
    return np.stack(o, axis=2).reshape(128, -1)
T, CK = 256, 48
def gates(g):
    t = np.zeros((128, 512), BF); t[:, :4 * N] = g
    return np.stack([t] * N)
def plus(g):
    return np.maximum(np.abs(g.astype(np.float32)), np.float32(0.0625)).astype(BF)
def apart(rng):
    g = np.zeros((128, 4 * N), BF)
    for e in range(N): g[8 * e:8 * e + 8, 4 * e:4 * e + 4] = plus(f(rng, 8, 4))
    return g
def setup_inputs(rng):
    return {"x": f(rng, N, 128, 4 * T), "wg": gates(f(rng, 128, 4 * N)), "w1": f(rng, N, 128, 2048)}
def setup_inputs_alike(rng):
    d = setup_inputs(rng); d["wg"] = gates(np.tile(f(rng, 128, 4), (1, N))); return d
def setup_inputs_ties(rng):
    d = setup_inputs(rng); d["wg"] = gates(plus(f(rng, 128, 4 * N))); d["x"] = -plus(d["x"])
    for s in range(N):
        k = rng.permutation(np.arange(T) // 5 if s % 2 else np.arange(T) % (T // (CK + 1)))
        d["x"][s] = d["x"][s].reshape(128, T, 4)[:, k].reshape(128, -1)
    return d
def setup_inputs_split(rng):
    d = setup_inputs(rng); g = apart(rng)
    v = d["x"].astype(np.float32).reshape(N, 128, T, 4)
    for s in range(N):
        p = rng.permutation(T)
        for e in range(N):
            sign = np.full((1, T, 1), -1, np.float32); sign[:, p[(e * CK + np.arange(CK)) % T]] = 1
            v[s, 8 * e:8 * e + 8] = np.abs(v[s, 8 * e:8 * e + 8]) * sign
    d["x"] = v.reshape(N, 128, 4 * T).astype(BF); d["wg"] = gates(g); return d
def setup_inputs_zeros(rng):
    d = setup_inputs(rng); g = apart(rng)
    v = d["x"].astype(np.float32).reshape(N, 128, T, 4)
    for s in range(N):
        for e in range(N):
            p = rng.permutation(T); u = np.abs(v[s, 8 * e:8 * e + 8])
            u[:, p[CK // 2:CK // 2 + CK]] = np.where(rng.random((8, CK, 4)) < 0.5, np.float32(-0.0), np.float32(0.0))
            u[:, p[CK // 2 + CK:]] *= np.float32(-1)
            v[s, 8 * e:8 * e + 8] = u
    d["x"] = v.reshape(N, 128, 4 * T).astype(BF); d["wg"] = gates(g); return d
def setup_inputs_spread(rng):
    d = setup_inputs(rng); d["x"] = wide(rng, N, 128, 4 * T, cols=6); return d
def check_inputs(d):
    b = []
    g = d["wg"].astype(np.float32)
    if (g != g[0]).any() or (g[:, :, 4 * N:] != 0).any(): b.append("wg")
    return b
def reference(x, wg, w1):
    took = []
    for s in range(N):
        z = mx_ref.matmul(mx_ref.quantize(wg[s]), mx_ref.quantize(x[s])) + np.float32(0.0)
        took.append([np.argsort(-z[e], kind="stable")[:CK] for e in range(N)])
    y = np.zeros((N, 128, T, 4), np.float32)
    for e in range(N):
        q = mx_ref.quantize(np.concatenate([cols(x[s], took[s][e]) for s in range(N)], axis=1))
        rs = [np.maximum(mx_ref.matmul(mx_ref.quantize(np.ascontiguousarray(cut(w1[e], i))), q), np.float32(0.0)) * np.float32(0.05) for i in range(4)]
        v = decode(mx_ref.quantize(tile(rs))).reshape(128, N, CK, 4)
        for s in range(N): y[s][:, took[s][e]] += v[:, s]
    return {"y": y.reshape(N, 128, 4 * T)}

@@ -1,0 +1,321 @@
+from concourse.bass import DstId, RemoteDMATransfer
+from concourse.mybir import dt, AluOpType as A, AxisListType, ActivationFunctionType as F
+
+N, TOK, CK = 8, 256, 48
+B4 = 4 * CK
+OWN = (N - 1) * CK
+ALLC = (2 * N - 1) * CK
+HALF = 4 * CK
+
+SCRATCH = {
+    "xs": ("sbuf", [128, 4 * TOK], "bfloat16"),
+    "wgs": ("sbuf", [128, 32], "bfloat16"),
+    "wr": ("sbuf", [128, 512], "bfloat16"),
+    "w1s": ("sbuf", [128, 2048], "bfloat16"),
+    "qx": ("sbuf", [128, TOK], "float8_e4m3fn_x4"), "sx": ("sbuf", [128, TOK], "uint8"),
+    "qr": ("sbuf", [128, 128], "float8_e4m3fn_x4"), "sr": ("sbuf", [128, 128], "uint8"),
+    "qw": ("sbuf", [128, 512], "float8_e4m3fn_x4"), "sw": ("sbuf", [128, 512], "uint8"),
+    "ones": ("sbuf", [128, 512], "bfloat16"),
+    "em": ("sbuf", [128, 2048], "bfloat16"),
+    "qe": ("sbuf", [128, 512], "float8_e4m3fn_x4"), "se": ("sbuf", [128, 512], "uint8"),
+    "ps": ("psum", [128, 4096], "float32"),
+    "pi": ("sbuf", [128, 4], "int32"), "bi": ("sbuf", [128, 12], "int32"), "bf": ("sbuf", [128, 12], "float32"),
+    "wgo": ("sbuf", [128, 32], "int32"), "wgu": ("sbuf", [128, 32], "uint16"),
+    "col": ("sbuf", [128, 272], "float32"), "val": ("sbuf", [128, TOK], "float32"),
+    "meq": ("sbuf", [128, 256], "float32"), "mne": ("sbuf", [128, 272], "float32"),
+    "mlt": ("sbuf", [128, 256], "bfloat16"), "mnb": ("sbuf", [128, 256], "bfloat16"),
+    "idw": ("sbuf", [128, 9 * B4], "float32"), "base": ("sbuf", [128, 128], "float32"),
+    "eix": ("sbuf", [128, 128], "float32"), "gm": ("sbuf", [128, 128], "float32"),
+    "m1": ("sbuf", [128, 272], "float32"), "fs": ("sbuf", [128, 272], "float32"),
+    "eq": ("sbuf", [128, 256], "bfloat16"), "eqm": ("sbuf", [128, 256], "bfloat16"), "eqs": ("sbuf", [128, 256], "bfloat16"),
+    "cmp": ("sbuf", [128, 4096], "bfloat16"), "acc": ("sbuf", [128, 16], "float32"),
+    "d2": ("sbuf", [128, 32], "float32"), "rku": ("sbuf", [128, 16], "uint16"),
+    "wa": ("sbuf", [128, 256], "float32"), "wb": ("sbuf", [128, 96], "float32"), "va": ("sbuf", [128, 96], "float32"),
+    "ca": ("sbuf", [128, 6], "float32"), "oa": ("sbuf", [128, 24], "float32"),
+    "of0": ("sbuf", [128, 24], "uint16"), "of1": ("sbuf", [128, 24], "uint16"),
+    "of2": ("sbuf", [128, 24], "uint16"), "of3": ("sbuf", [128, 24], "uint16"),
+    "xt": ("sbuf", [128, 4 * N * CK], "bfloat16"),
+    "sb": ("sbuf", [128, ALLC], "float8_e4m3fn_x4"), "ss": ("sbuf", [128, ALLC], "uint8"),
+    "ht": ("sbuf", [128, 4 * N * CK], "bfloat16"),
+    "rb": ("sbuf", [128, ALLC], "float8_e4m3fn_x4"), "rs": ("sbuf", [128, ALLC], "uint8"),
+    "x1": ("sbuf", [128, 32], "float32"), "yb": ("sbuf", [128, 64], "float32"), "x2": ("sbuf", [128, 64], "float32"),
+    "c2": ("sbuf", [128, 32], "float32"), "rka": ("sbuf", [128, 128], "float32"),
+    "tk": ("sbuf", [128, 128], "float32"), "pb": ("sbuf", [128, 128], "float32"), "tp": ("sbuf", [128, 128], "float32"),
+    "km": ("sbuf", [128, 128], "float32"),
+    "l1": ("sbuf", [128, 64], "float32"), "l2": ("sbuf", [128, 32], "float32"), "l3": ("sbuf", [128, 16], "float32"),
+    "k1": ("sbuf", [128, 64], "float32"), "k2": ("sbuf", [128, 32], "float32"), "k3": ("sbuf", [128, 16], "uint16"),
+    "k4": ("sbuf", [128, 16], "float32"),
+    "row": ("sbuf", [128, 256], "float32"), "wc": ("sbuf", [128, 256], "float32"), "wd": ("sbuf", [128, 96], "float32"),
+    "vc": ("sbuf", [128, 96], "float32"), "cc": ("sbuf", [128, 6], "float32"), "oc": ("sbuf", [128, 24], "float32"),
+    "po": ("sbuf", [128, 96], "uint16"), "lb": ("sbuf", [128, 64], "uint16"),
+    "vv": ("sbuf", [128, N * B4], "float32"), "pp": ("sbuf", [128, (N + 1) * B4], "float32"),
+    "yo": ("sbuf", [128, 4 * TOK], "float32"),
+}
+SEMAPHORES = ["v", "s", "t", "p", "dwg", "dx", "dw1", "dy", "a1A", "a1B", "a2A", "a2B", "loc"]
+
+
+def rank_program(g, core, T, topo):
+    rank = T.rank_of(core)
+    if rank is None:
+        return
+    Q = {"v": g.vector, "s": g.scalar, "t": g.tensor, "p": g, "y": g.sync}
+    cnt = {"v": 0, "s": 0, "t": 0, "p": 0}
+    known = {}
+
+    def need(q, *deps):
+        best = {}
+        for d in deps:
+            if d is None:
+                continue
+            for sem, val in (d if isinstance(d, list) else [d]):
+                best[sem] = max(best.get(sem, 0), val)
+        for sem, val in best.items():
+            if known.get((q, sem), 0) < val:
+                Q[q].wait_ge(T.sem[sem], val)
+                known[(q, sem)] = val
+
+    def run(q, fn, *deps):
+        need(q, *deps)
+        cnt[q] += 1
+        fn().then_inc(T.sem[q], 1)
+        return (q, cnt[q])
+
+    V, S = g.vector, g.scalar
+
+    def cp(q, out, in_, *deps):
+        if q == "v":
+            return run("v", lambda: V.tensor_copy(out, in_), *deps)
+        return run("s", lambda: S.activation(out, in_, F.Copy), *deps)
+
+    def ts(out, in0, s1, op0, *deps):
+        return run("v", lambda: V.tensor_scalar(out, in0, s1, None, op0), *deps)
+
+    def tt(out, a, b, op, *deps):
+        return run("v", lambda: V.tensor_tensor(out, a, b, op), *deps)
+
+    g.sync.dma_start(T.wgs[:, 0:32], T.wg[:, 0:32]).then_inc(T.sem.dwg, 16)
+    g.sync.dma_start(T.xs[:, :], T.x[:, :]).then_inc(T.sem.dx, 16)
+    g.sync.dma_start(T.w1s[:, :], T.w1[:, :]).then_inc(T.sem.dw1, 16)
+
+    i_pi = run("p", lambda: g.iota(T.pi[:, 0:1], [[0, 1]], 0, 1))
+    i_wgo = run("p", lambda: g.iota(T.wgo[:, :], [[4, 8], [0, 4]], 0, 0))
+    i_col = run("p", lambda: g.iota(T.col[:, :], [[0, 17], [1, 16]], 0, 0, allow_small_or_imprecise_dtypes=True))
+    i_val = run("p", lambda: g.iota(T.val[:, :], [[4, TOK]], 0, 0, allow_small_or_imprecise_dtypes=True))
+    c_one = run("v", lambda: V.memset(T.ones[:, :], 1.0))
+    i_em = None
+    for b in range(4):
+        i_em = run("p", lambda: g.affine_select(T.em[:, 512 * b:512 * b + 512], T.ones[:, :], [[-1, 512]], A.is_equal, 0.0, b, 4), c_one)
+    i_base = run("p", lambda: g.iota(T.base[:, :], [[B4, 8], [0, 16]], B4, 0, allow_small_or_imprecise_dtypes=True))
+    i_eix = run("p", lambda: g.iota(T.eix[:, :], [[1, 8], [0, 16]], 0, 0, allow_small_or_imprecise_dtypes=True))
+    i_idw = run("p", lambda: g.iota(T.idw[:, :], [[1, 9 * B4]], 0, 0, allow_small_or_imprecise_dtypes=True))
+
+    c3 = ts(T.bi[:, 0:1], T.pi[:, 0:1], 3, A.bitwise_and, i_pi)
+    c15 = ts(T.bi[:, 4:5], T.pi[:, 0:1], 15, A.bitwise_and, i_pi)
+    cg = ts(T.bi[:, 8:9], T.pi[:, 0:1], 4, A.arith_shift_right, i_pi)
+    f3 = cp("v", T.bf[:, 0:1], T.bi[:, 0:1], c3)
+    f15 = cp("v", T.bf[:, 4:5], T.bi[:, 4:5], c15)
+    fg = cp("v", T.bf[:, 8:9], T.bi[:, 8:9], cg)
+    c_wgu = ts(T.wgu[:, :], T.wgo[:, :], T.bf[:, 0:1], A.add, i_wgo, f3)
+    R = T.bf[:, 4:5]
+    c_meq = ts(T.meq[:, :], T.col[:, 0:256], R, A.is_equal, i_col, f15)
+    c_mne = ts(T.mne[:, :], T.col[:, :], R, A.not_equal)
+    c_mlt = ts(T.mlt[:, :], T.col[:, 0:256], R, A.is_lt)
+    c_mnb = ts(T.mnb[:, :], T.col[:, 0:256], 0.0, A.not_equal)
+    c_m1 = run("v", lambda: V.memset(T.m1[:, 256:272], 0.0))
+    c_pp = run("v", lambda: V.memset(T.pp[:, 0:B4], 0.0))
+
+    k_wr = cp("s", T.wr[:, :], T.wgs[:, 0:32].indirect(T.wgu[:, 0:32]), ("dwg", 16), c_wgu)
+    k_qr = run("v", lambda: V.quantize_mx(T.qr[:, :], T.sr[:, :], T.wr[:, :]), k_wr)
+    k_qx = run("v", lambda: V.quantize_mx(T.qx[:, :], T.sx[:, :], T.xs[:, :]), ("dx", 16))
+    Z = T.ps[:, 3584:3584 + TOK]
+    k_z = run("t", lambda: g.tensor.matmul_mx(Z, T.qr[:, :], T.sr[:, :], T.qx[:, :], T.sx[:, :], True, True), k_qr, k_qx)
+
+    k_m1 = tt(T.m1[:, 0:256], Z, T.meq[:, :], A.mult, k_z, c_meq)
+    k_fs = run("v", lambda: V.tensor_tensor_scan(T.fs[:, :], T.mne[:, :], T.m1[:, :], 0.0, A.mult, A.add), k_m1, c_m1, c_mne)
+    k_acc = None
+    for i in range(15, -1, -1):
+        own = T.fs[:, 16 * i + 15:16 * i + 16]
+        k = None
+        if i:
+            k = ts(T.cmp[:, 256 * i:256 * i + 16 * i], T.ps[:, 3584:3584 + 16 * i], own, A.is_ge, k_fs)
+        k = ts(T.cmp[:, 256 * i + 16 * i:256 * i + 256], T.ps[:, 3584 + 16 * i:3584 + 256], own, A.is_gt, k_fs)
+        row = T.cmp[:, 256 * i:256 * i + 256]
+        k_acc = run("s", lambda: S.activation(row, row, F.Copy, accum_out=T.acc[:, i:i + 1]), k)
+        if i == 8:
+            k_eq = tt(T.eq[:, :], Z, T.fs[:, 16:272], A.is_equal, k_fs)
+            k_eqm = tt(T.eqm[:, :], T.eq[:, :], T.mlt[:, :], A.mult, k_eq, c_mlt)
+            k_eqs = run("v", lambda: V.tensor_tensor_scan(T.eqs[:, :], T.mnb[:, :], T.eqm[:, :], 0.0, A.mult, A.add), k_eqm, c_mnb)
+    k_rk = tt(T.d2[:, 0:16], T.acc[:, :], T.eqs[:, 15:256:16], A.add, k_acc, k_eqs)
+    k_rku = cp("v", T.rku[:, :], T.d2[:, 0:16], k_rk)
+
+    def spread(C, O, w, kc, pk, qs):
+        ks = []
+        n = 0
+        for q in range(4):
+            for d in (q, q ^ 1):
+                o = 2 * w * (q ^ pk)
+                ks.append(cp(qs[n % len(qs)], O[32 * d:32 * d + 32, o:o + 2 * w], C[32 * q:32 * q + 32, :], kc))
+                n += 1
+        ks2 = list(ks)
+        for h in range(2):
+            o = 4 * w * (h ^ (pk >> 1))
+            ks2.append(cp(qs[h % len(qs)], O[64 * (1 - h):64 * (1 - h) + 64, o:o + 4 * w], O[64 * h:64 * h + 64, o:o + 4 * w], ks))
+        return ks2
+
+    def lists(W, W2, VT, C, O, kw, flip, pk, qs):
+        ks = []
+        n = 0
+        for m in range(3):
+            for h in range(2):
+                ks.append(cp(qs[n % len(qs)], W2[:, 32 * m + 16 * h:32 * m + 16 * h + 16], W[:, 16 * m:16 * m + 16], kw))
+                n += 1
+        kt = run("v", lambda: V.transpose(VT[:, :], W2[:, :]), ks)
+        kc = [cp(qs[e % len(qs)], C[:, 3 * (e ^ flip):3 * (e ^ flip) + 3], VT[:, 16 * e:96:32], kt) for e in range(2)]
+        return spread(C, O, 3, kc, pk, qs)
+
+    k_wa = cp("v", T.wa[:, 0:256].indirect(T.rku[:, 0:16]), T.val[:, :], k_rku, i_val)
+    k_oa = lists(T.wa, T.wb, T.va, T.ca, T.oa, k_wa, (rank & 1) ^ 1, (rank >> 1) ^ 3, "vs")
+    k_of = [ts(T["of%d" % t][:, :], T.oa[:, :], float(t), A.add, k_oa) for t in (2, 0, 3, 1)]
+    k_of = {2: k_of[0], 0: k_of[1], 3: k_of[2], 1: k_of[3]}
+    k_q1 = []
+    for c in range(2):
+        ks = []
+        for t in (2, 0, 3, 1):
+            ks.append(cp("vs"[t // 2], T.xt[:, 4 * HALF * c + t:4 * HALF * (c + 1):4], T.xs[:, :].indirect(T["of%d" % t][:, 12 * c:12 * c + 12]), k_of[t], ("dx", 16)))
+        o = HALF * c
+        k_q1.append(run("v", lambda: V.quantize_mx(T.sb[:, o:o + HALF], T.ss[:, o:o + HALF], T.xt[:, 4 * o:4 * o + 4 * HALF]), ks))
+
+    loc = [0]
+
+    def send(dels, src_col, dst_col, codes, plane, sem):
+        per = 8 // (4 if len(dels) > 2 else len(dels))
+        for view in ("q", "s"):
+            tr = []
+            for j, de in enumerate(dels):
+                dst = T.cores[rank ^ de]
+                eng = topo.engines(core, dst)
+                mask = sum(1 << e for e in eng[j * per:(j + 1) * per])
+                rid, pid = topo.addr(dst, core)
+                a, b = src_col(de), dst_col(de)
+                if view == "q":
+                    sa, da = codes[:, a:a + CK].bitcast(dt.uint8), codes[:, b:b + CK].bitcast(dt.uint8)
+                else:
+                    sa, da = plane[:, a:a + CK], plane[:, b:b + CK]
+                tr.append(RemoteDMATransfer(dst_ids=[DstId(rid=rid, pnc=pid)], dma_engine_mask=mask, remote_sem=T.sem[sem], src=sa, dst=da))
+                loc[0] += per
+            g.remote_dma_fused(tr, local_sem=T.sem.loc)
+        return 2 * per * len(dels)
+
+    FAR, NEAR = (7, 6, 5, 4), (3, 2, 1)
+    out1, in1 = (lambda de: CK * (7 - de)), (lambda de: OWN + CK * de)
+    need("p", k_q1[0])
+    nA = send(FAR, out1, in1, T.sb, T.ss, "a1A")
+    need("p", k_q1[1])
+    nB = send(NEAR, out1, in1, T.sb, T.ss, "a1B")
+
+    k_qw = run("v", lambda: V.quantize_mx(T.qw[:, :], T.sw[:, :], T.w1s[:, :]), ("dw1", 16))
+    k_qe = run("v", lambda: V.quantize_mx(T.qe[:, :], T.se[:, :], T.em[:, :]), i_em)
+    k = cp("s", T.d2[:, 16:32], T.d2[:, 0:16], k_rk)
+    k = run("v", lambda: V.transpose(T.x1[:, :], T.d2[:, :]), k)
+    ks = [cp("vs"[h], T.yb[:, 32 * h + 16 * j:32 * h + 16 * j + 16], T.x1[:, 16 * h:16 * h + 16], k) for h in range(2) for j in range(2)]
+    k = run("v", lambda: V.transpose(T.x2[:, :], T.yb[:, :]), ks)
+    ks = [cp("vs"[h], T.c2[:, 16 * h:16 * h + 16], T.x2[:, 32 * h:32 * h + 16], k) for h in range(2)]
+    ks = spread(T.c2, T.rka, 16, ks, 0, "vs")
+    k_tk = ts(T.tk[:, :], T.rka[:, :], float(CK), A.is_lt, ks)
+    k_pb = tt(T.pb[:, :], T.rka[:, :], T.base[:, :], A.add, i_base)
+    k_gm = ts(T.gm[:, :], T.eix[:, :], T.bf[:, 8:9], A.is_lt, i_eix, fg)
+    k_tp = tt(T.tp[:, :], T.tk[:, :], T.pb[:, :], A.mult, k_tk, k_pb)
+    k_km = tt(T.km[:, :], T.tp[:, :], T.gm[:, :], A.mult, k_tp, k_gm)
+    kl1 = tt(T.l1[:, :], T.tp[:, 0:64], T.tp[:, 64:128], A.max, k_tp)
+    kk1 = tt(T.k1[:, :], T.km[:, 0:64], T.km[:, 64:128], A.max, k_km)
+    kl2 = tt(T.l2[:, :], T.l1[:, 0:32], T.l1[:, 32:64], A.max, kl1)
+    kk2 = tt(T.k2[:, :], T.k1[:, 0:32], T.k1[:, 32:64], A.max, kk1)
+    kl3 = tt(T.l3[:, :], T.l2[:, 0:16], T.l2[:, 16:32], A.max, kl2)
+    kk3 = tt(T.k4[:, :], T.k2[:, 0:16], T.k2[:, 16:32], A.max, kk2)
+    kk4 = cp("v", T.k3[:, :], T.k4[:, :], kk3)
+    k_lb = [ts(T.lb[:, 16 * b:16 * b + 16], T.l3[:, :], float(CK * b), A.add, kl3) for b in range(4)]
+
+    out2, in2 = (lambda de: OWN + CK * de), (lambda de: CK * (7 - de))
+    arr1 = [("a1A", nA), ("a1B", nB)]
+    rb_free = {}
+    k_r = {}
+    for c in range(2):
+        col = OWN + HALF * (1 - c)
+        for i in range(4):
+            bank = 4 * c + i
+            k_r[(c, i)] = run("t", lambda: g.tensor.matmul_mx(T.ps[:, 512 * bank:512 * bank + HALF], T.qw[:, 128 * i:128 * i + 128], T.sw[:, 128 * i:128 * i + 128],
+                                                  T.sb[:, col:col + HALF], T.ss[:, col:col + HALF], True, True),
+                               arr1[c], k_qw, k_q1[1] if c else None, k_rku)
+    k_q2 = []
+    for c in range(2):
+        o = 4 * HALF * (1 - c)
+        ks = []
+        for i in range(4):
+            bank = 4 * c + i
+            out, src = T.ht[:, o + i:o + 4 * HALF:4], T.ps[:, 512 * bank:512 * bank + HALF]
+            if i % 2 == 0:
+                kk = run("s", lambda: S.activation(out, src, F.Relu, scale=0.05), k_r[(c, i)])
+            else:
+                kk = run("v", lambda: V.tensor_scalar(out, src, 0.0, 0.05, A.max, A.mult), k_r[(c, i)])
+            ks.append(kk)
+            rb_free[bank] = kk
+        col = OWN + HALF * (1 - c)
+        k_q2.append(run("v", lambda: V.quantize_mx(T.rb[:, col:col + HALF], T.rs[:, col:col + HALF], T.ht[:, o:o + 4 * HALF]), ks))
+        need("p", k_q2[c])
+        n2 = send((FAR, NEAR)[c], out2, in2, T.rb, T.rs, ("a2A", "a2B")[c])
+        if c == 0:
+            mA = n2
+        else:
+            mB = n2
+
+    k = cp("v", T.row[:, :], T.idw[:, :].indirect(T.k3[:, 0:16]), kk4, i_idw)
+    k_wc = cp("v", T.wc[:, 0:256].indirect(T.rku[:, 0:16]), T.row[:, :], k)
+    k_oc = lists(T.wc, T.wd, T.vc, T.cc, T.oc, k_wc, 0, 0, "vs")
+    k_po = None
+    for b in range(4):
+        for m in range(3):
+            k_po = ts(T.po[:, 3 * b + m:96:12], T.oc[:, m:24:3], float(CK * b), A.add, k_oc)
+
+    arr2 = [("a2A", mA), ("a2B", mB)]
+    k_d = {}
+    for c in range(2):
+        for b in range(4):
+            bank = 4 * c + b
+            k_d[(c, b)] = run("t", lambda: g.tensor.matmul_mx(T.ps[:, 512 * bank:512 * bank + HALF], T.qe[:, 128 * b:128 * b + 128], T.se[:, 128 * b:128 * b + 128],
+                                                  T.rb[:, HALF * c:HALF * c + HALF], T.rs[:, HALF * c:HALF * c + HALF], True, True),
+                               arr2[c], k_qe, rb_free[bank], k_q2[1] if c else None)
+    done = {}
+    nxt = [0]
+    k_p = {-1: c_pp}
+    for c in range(2):
+        exps = sorted(e for e in range(N) if (e ^ rank ^ 7) // 4 == c)
+        for e in exps:
+            d = (e ^ rank ^ 7) % 4
+            ks = []
+            for b in (1, 0, 2, 3):
+                q = "s" if b else "v"
+                if c == 0 and b == 1:
+                    q = "v"
+                bank = 4 * c + b
+                src = T.ps[:, 512 * bank + CK * d:512 * bank + CK * d + CK]
+                dst = T.vv[:, B4 * e + CK * b:B4 * e + CK * b + CK] if e else T.pp[:, B4 + CK * b:B4 + CK * b + CK]
+                ks.append(cp(q, dst, src, k_d[(c, b)]))
+            done[e] = ks
+        while nxt[0] in done:
+            e = nxt[0]
+            if e == 0:
+                k_p[0] = done[0]
+            else:
+                k_p[e] = run("v", lambda: V.tensor_tensor(T.pp[:, B4 * (e + 1):B4 * (e + 2)], T.pp[:, 0:B4 * (e + 1)].indirect(T.po[:, 12 * e:12 * e + 12]),
+                                                          T.vv[:, B4 * e:B4 * e + B4], A.add), k_p[e - 1], done[e], k_po, c_pp)
+            nxt[0] += 1
+    ny = 0
+    for h in range(2):
+        ks = []
+        for b in (2, 0, 3, 1):
+            ks.append(cp("vs"[b // 2], T.yo[:, 512 * h + b:512 * (h + 1):4], T.pp[:, :].indirect(T.lb[:, 16 * b + 8 * h:16 * b + 8 * h + 8]), k_p[7], k_lb[b]))
+        need("y", ks)
+        g.sync.dma_start(T.y[:, 512 * h:512 * h + 512], T.yo[:, 512 * h:512 * h + 512]).then_inc(T.sem.dy, 16)
+        ny += 16
+    need("y", ("dy", ny))
+    need("p", [("v", cnt["v"]), ("s", cnt["s"]), ("t", cnt["t"]), ("p", cnt["p"]), ("loc", loc[0])])

@@ -6,9 +6,14 @@ B4 = 4 * CK
 OWN = (N - 1) * CK
 ALLC = (2 * N - 1) * CK
 HALF = 4 * CK
+NV = 2
+ULP = 2.0 ** -24 * (1 + 2.0 ** -6)
+TINY = 2.0 ** -124
 
 SCRATCH = {
     "xs": ("sbuf", [128, 4 * TOK], "bfloat16"),
+    "xs1": ("sbuf", [128, 4 * TOK + 16], "bfloat16"), "xs2": ("sbuf", [128, 4 * TOK + 16], "bfloat16"),
+    "xs3": ("sbuf", [128, 4 * TOK + 16], "bfloat16"),
     "wgs": ("sbuf", [128, 32], "bfloat16"),
     "wr": ("sbuf", [128, 512], "bfloat16"),
     "w1s": ("sbuf", [128, 2048], "bfloat16"),
@@ -19,39 +24,38 @@ SCRATCH = {
     "em": ("sbuf", [128, 2048], "bfloat16"),
     "qe": ("sbuf", [128, 512], "float8_e4m3fn_x4"), "se": ("sbuf", [128, 512], "uint8"),
     "ps": ("psum", [128, 4096], "float32"),
-    "pi": ("sbuf", [128, 4], "int32"), "bi": ("sbuf", [128, 12], "int32"), "bf": ("sbuf", [128, 12], "float32"),
+    "pi": ("sbuf", [128, 4], "int32"), "bi": ("sbuf", [128, 4], "int32"), "bf": ("sbuf", [128, 4], "float32"),
+    "bp": ("sbuf", [128, 4], "float32"),
     "wgo": ("sbuf", [128, 32], "int32"), "wgu": ("sbuf", [128, 32], "uint16"),
-    "col": ("sbuf", [128, 272], "float32"), "val": ("sbuf", [128, TOK], "float32"),
-    "meq": ("sbuf", [128, 256], "float32"), "mne": ("sbuf", [128, 272], "float32"),
-    "mlt": ("sbuf", [128, 256], "bfloat16"), "mnb": ("sbuf", [128, 256], "bfloat16"),
-    "idw": ("sbuf", [128, 9 * B4], "float32"), "base": ("sbuf", [128, 128], "float32"),
+    "col": ("sbuf", [128, 256], "float32"), "val": ("sbuf", [128, TOK], "float32"),
+    "meq": ("sbuf", [128, 256], "float32"), "mne": ("sbuf", [128, 256], "float32"), "mnb": ("sbuf", [128, 256], "bfloat16"),
+    "idw": ("sbuf", [128, 9 * B4], "float32"),
     "eix": ("sbuf", [128, 128], "float32"), "gm": ("sbuf", [128, 128], "float32"),
-    "m1": ("sbuf", [128, 272], "float32"), "fs": ("sbuf", [128, 272], "float32"),
-    "eq": ("sbuf", [128, 256], "bfloat16"), "eqm": ("sbuf", [128, 256], "bfloat16"), "eqs": ("sbuf", [128, 256], "bfloat16"),
-    "cmp": ("sbuf", [128, 4096], "bfloat16"), "acc": ("sbuf", [128, 16], "float32"),
-    "d2": ("sbuf", [128, 32], "float32"), "rku": ("sbuf", [128, 16], "uint16"),
-    "wa": ("sbuf", [128, 256], "float32"), "wb": ("sbuf", [128, 96], "float32"), "va": ("sbuf", [128, 96], "float32"),
-    "ca": ("sbuf", [128, 6], "float32"), "oa": ("sbuf", [128, 24], "float32"),
-    "of0": ("sbuf", [128, 24], "uint16"), "of1": ("sbuf", [128, 24], "uint16"),
-    "of2": ("sbuf", [128, 24], "uint16"), "of3": ("sbuf", [128, 24], "uint16"),
+    "m1": ("sbuf", [128, 256], "float32"), "fs": ("sbuf", [128, 256], "float32"),
+    "ulp": ("sbuf", [128, 256], "float32"), "zz": ("sbuf", [128, 512], "float32"),
+    "eq": ("sbuf", [128, 256], "bfloat16"), "eqs": ("sbuf", [128, 256], "bfloat16"),
+    "cmp": ("sbuf", [128, 16, 264], "bfloat16"), "cv": ("sbuf", [128, NV, 264], "bfloat16"), "acc": ("sbuf", [128, 16], "float32"),
+    "rku": ("sbuf", [128, 16], "uint16"),
+    "wa": ("sbuf", [128, 256], "float32"), "wb": ("sbuf", [128, 3, 32], "float32"), "va": ("sbuf", [128, 96], "float32"),
+    "ca": ("sbuf", [128, 6], "float32"), "oa": ("sbuf", [128, 24], "float32"), "of": ("sbuf", [128, 24], "uint16"),
     "xt": ("sbuf", [128, 4 * N * CK], "bfloat16"),
     "sb": ("sbuf", [128, ALLC], "float8_e4m3fn_x4"), "ss": ("sbuf", [128, ALLC], "uint8"),
     "ht": ("sbuf", [128, 4 * N * CK], "bfloat16"),
     "rb": ("sbuf", [128, ALLC], "float8_e4m3fn_x4"), "rs": ("sbuf", [128, ALLC], "uint8"),
+    "tk": ("sbuf", [128, 16], "float32"), "pb": ("sbuf", [128, 16], "float32"), "d2": ("sbuf", [128, 32], "float32"),
     "x1": ("sbuf", [128, 32], "float32"), "yb": ("sbuf", [128, 64], "float32"), "x2": ("sbuf", [128, 64], "float32"),
-    "c2": ("sbuf", [128, 32], "float32"), "rka": ("sbuf", [128, 128], "float32"),
-    "tk": ("sbuf", [128, 128], "float32"), "pb": ("sbuf", [128, 128], "float32"), "tp": ("sbuf", [128, 128], "float32"),
+    "c2": ("sbuf", [128, 32], "float32"), "tp": ("sbuf", [128, 128], "float32"),
     "km": ("sbuf", [128, 128], "float32"),
     "l1": ("sbuf", [128, 64], "float32"), "l2": ("sbuf", [128, 32], "float32"), "l3": ("sbuf", [128, 16], "float32"),
     "k1": ("sbuf", [128, 64], "float32"), "k2": ("sbuf", [128, 32], "float32"), "k3": ("sbuf", [128, 16], "uint16"),
     "k4": ("sbuf", [128, 16], "float32"),
-    "row": ("sbuf", [128, 256], "float32"), "wc": ("sbuf", [128, 256], "float32"), "wd": ("sbuf", [128, 96], "float32"),
+    "row": ("sbuf", [128, 256], "float32"), "wc": ("sbuf", [128, 256], "float32"), "wd": ("sbuf", [128, 3, 32], "float32"),
     "vc": ("sbuf", [128, 96], "float32"), "cc": ("sbuf", [128, 6], "float32"), "oc": ("sbuf", [128, 24], "float32"),
     "po": ("sbuf", [128, 96], "uint16"), "lb": ("sbuf", [128, 64], "uint16"),
-    "vv": ("sbuf", [128, N * B4], "float32"), "pp": ("sbuf", [128, (N + 1) * B4], "float32"),
+    "vv": ("sbuf", [128, N, B4], "float32"), "pp": ("sbuf", [128, (N + 1) * B4], "float32"),
     "yo": ("sbuf", [128, 4 * TOK], "float32"),
 }
-SEMAPHORES = ["v", "s", "t", "p", "dwg", "dx", "dw1", "dy", "a1A", "a1B", "a2A", "a2B", "loc"]
+SEMAPHORES = ["v", "s", "t", "p", "dwg", "dx", "dxs", "dw1", "dy", "a1A", "a1B", "a2A", "a2B", "loc"]
 
 
 def rank_program(g, core, T, topo):
@@ -93,60 +97,65 @@ def rank_program(g, core, T, topo):
     def tt(out, a, b, op, *deps):
         return run("v", lambda: V.tensor_tensor(out, a, b, op), *deps)
 
-    g.sync.dma_start(T.wgs[:, 0:32], T.wg[:, 0:32]).then_inc(T.sem.dwg, 16)
     g.sync.dma_start(T.xs[:, :], T.x[:, :]).then_inc(T.sem.dx, 16)
+    g.scalar.dma_start(T.wgs[:, 0:32], T.wg[:, 0:32]).then_inc(T.sem.dwg, 16)
+    g.sync.wait_ge(T.sem.dx, 16)
+    for t in range(1, 4):
+        g.sync.dma_start(T["xs%d" % t][:, 16 - t:16 - t + 4 * TOK], T.x[:, :]).then_inc(T.sem.dxs, 16)
     g.sync.dma_start(T.w1s[:, :], T.w1[:, :]).then_inc(T.sem.dw1, 16)
 
     i_pi = run("p", lambda: g.iota(T.pi[:, 0:1], [[0, 1]], 0, 1))
     i_wgo = run("p", lambda: g.iota(T.wgo[:, :], [[4, 8], [0, 4]], 0, 0))
-    i_col = run("p", lambda: g.iota(T.col[:, :], [[0, 17], [1, 16]], 0, 0, allow_small_or_imprecise_dtypes=True))
+    i_col = run("p", lambda: g.iota(T.col[:, :], [[0, 16], [1, 16]], 0, 0, allow_small_or_imprecise_dtypes=True))
     i_val = run("p", lambda: g.iota(T.val[:, :], [[4, TOK]], 0, 0, allow_small_or_imprecise_dtypes=True))
     c_one = run("v", lambda: V.memset(T.ones[:, :], 1.0))
     i_em = None
     for b in range(4):
         i_em = run("p", lambda: g.affine_select(T.em[:, 512 * b:512 * b + 512], T.ones[:, :], [[-1, 512]], A.is_equal, 0.0, b, 4), c_one)
-    i_base = run("p", lambda: g.iota(T.base[:, :], [[B4, 8], [0, 16]], B4, 0, allow_small_or_imprecise_dtypes=True))
     i_eix = run("p", lambda: g.iota(T.eix[:, :], [[1, 8], [0, 16]], 0, 0, allow_small_or_imprecise_dtypes=True))
     i_idw = run("p", lambda: g.iota(T.idw[:, :], [[1, 9 * B4]], 0, 0, allow_small_or_imprecise_dtypes=True))
 
-    c3 = ts(T.bi[:, 0:1], T.pi[:, 0:1], 3, A.bitwise_and, i_pi)
-    c15 = ts(T.bi[:, 4:5], T.pi[:, 0:1], 15, A.bitwise_and, i_pi)
-    cg = ts(T.bi[:, 8:9], T.pi[:, 0:1], 4, A.arith_shift_right, i_pi)
-    f3 = cp("v", T.bf[:, 0:1], T.bi[:, 0:1], c3)
-    f15 = cp("v", T.bf[:, 4:5], T.bi[:, 4:5], c15)
-    fg = cp("v", T.bf[:, 8:9], T.bi[:, 8:9], cg)
-    c_wgu = ts(T.wgu[:, :], T.wgo[:, :], T.bf[:, 0:1], A.add, i_wgo, f3)
-    R = T.bf[:, 4:5]
-    c_meq = ts(T.meq[:, :], T.col[:, 0:256], R, A.is_equal, i_col, f15)
+    cb = [ts(T.bi[:, 0:1], T.pi[:, 0:1], 3, A.bitwise_and, i_pi),
+          ts(T.bi[:, 1:2], T.pi[:, 0:1], 15, A.bitwise_and, i_pi),
+          ts(T.bi[:, 2:3], T.pi[:, 0:1], 4, A.arith_shift_right, i_pi)]
+    c_bf = cp("v", T.bf[:, 0:3], T.bi[:, 0:3], cb)
+    c_wgu = ts(T.wgu[:, :], T.wgo[:, :], T.bf[:, 0:1], A.add, i_wgo, c_bf)
+    R = T.bf[:, 1:2]
+    c_meq = ts(T.meq[:, :], T.col[:, :], R, A.is_equal, i_col, c_bf)
     c_mne = ts(T.mne[:, :], T.col[:, :], R, A.not_equal)
-    c_mlt = ts(T.mlt[:, :], T.col[:, 0:256], R, A.is_lt)
-    c_mnb = ts(T.mnb[:, :], T.col[:, 0:256], 0.0, A.not_equal)
-    c_m1 = run("v", lambda: V.memset(T.m1[:, 256:272], 0.0))
-    c_pp = run("v", lambda: V.memset(T.pp[:, 0:B4], 0.0))
 
     k_wr = cp("s", T.wr[:, :], T.wgs[:, 0:32].indirect(T.wgu[:, 0:32]), ("dwg", 16), c_wgu)
     k_qr = run("v", lambda: V.quantize_mx(T.qr[:, :], T.sr[:, :], T.wr[:, :]), k_wr)
     k_qx = run("v", lambda: V.quantize_mx(T.qx[:, :], T.sx[:, :], T.xs[:, :]), ("dx", 16))
-    Z = T.ps[:, 3584:3584 + TOK]
+    Z, Z2 = T.ps[:, 3584:3584 + TOK], T.ps[:, 3072:3072 + TOK]
+    k_z2 = run("t", lambda: g.tensor.matmul_mx(Z2, T.qr[:, :], T.sr[:, :], T.qx[:, :], T.sx[:, :], True, True), k_qr, k_qx)
     k_z = run("t", lambda: g.tensor.matmul_mx(Z, T.qr[:, :], T.sr[:, :], T.qx[:, :], T.sx[:, :], True, True), k_qr, k_qx)
+    c_mnb = ts(T.mnb[:, :], T.col[:, :], R, A.not_equal)
 
-    k_m1 = tt(T.m1[:, 0:256], Z, T.meq[:, :], A.mult, k_z, c_meq)
-    k_fs = run("v", lambda: V.tensor_tensor_scan(T.fs[:, :], T.mne[:, :], T.m1[:, :], 0.0, A.mult, A.add), k_m1, c_m1, c_mne)
+    k_ulp = run("s", lambda: S.activation(T.ulp[:, :], Z2, F.Abs, bias=TINY, scale=ULP), k_z2)
+    k_zc = cp("s", T.zz[:, 0:256], Z2, k_z2)
+    k_m1 = tt(T.m1[:, :], Z, T.meq[:, :], A.mult, k_z, c_meq)
+    k_fs = run("v", lambda: V.tensor_tensor_scan(T.fs[:, :], T.mne[:, :], T.m1[:, :], 0.0, A.mult, A.add), k_m1, c_mne)
+    k_zn = tt(T.zz[:, 256:512], Z, T.ulp[:, :], A.add, k_ulp)
+    k_eq = tt(T.eq[:, :], Z, T.fs[:, :], A.is_equal, k_fs)
+    k_eqs = run("v", lambda: V.tensor_tensor_scan(T.eqs[:, :], T.mnb[:, :], T.eq[:, :], 0.0, A.mult, A.subtract), k_eq, c_mnb)
+    k_ext = None
     k_acc = None
-    for i in range(15, -1, -1):
+    k_cv = []
+    for i in range(16):
         own = T.fs[:, 16 * i + 15:16 * i + 16]
-        k = None
-        if i:
-            k = ts(T.cmp[:, 256 * i:256 * i + 16 * i], T.ps[:, 3584:3584 + 16 * i], own, A.is_ge, k_fs)
-        k = ts(T.cmp[:, 256 * i + 16 * i:256 * i + 256], T.ps[:, 3584 + 16 * i:3584 + 256], own, A.is_gt, k_fs)
-        row = T.cmp[:, 256 * i:256 * i + 256]
-        k_acc = run("s", lambda: S.activation(row, row, F.Copy, accum_out=T.acc[:, i:i + 1]), k)
-        if i == 8:
-            k_eq = tt(T.eq[:, :], Z, T.fs[:, 16:272], A.is_equal, k_fs)
-            k_eqm = tt(T.eqm[:, :], T.eq[:, :], T.mlt[:, :], A.mult, k_eq, c_mlt)
-            k_eqs = run("v", lambda: V.tensor_tensor_scan(T.eqs[:, :], T.mnb[:, :], T.eqm[:, :], 0.0, A.mult, A.add), k_eqm, c_mnb)
-    k_rk = tt(T.d2[:, 0:16], T.acc[:, :], T.eqs[:, 15:256:16], A.add, k_acc, k_eqs)
-    k_rku = cp("v", T.rku[:, :], T.d2[:, 0:16], k_rk)
+        k = ts(T.cmp[:, i, 0:256], T.zz[:, 16 * i + 16:16 * i + 272], own, A.is_gt, k_zc, k_zn)
+        if i == 0:
+            k_ext = cp("v", T.cmp[:, :, 256], T.eqs[:, 15:256:16], k_eqs)
+        row = T.cmp[:, i, 0:257]
+        if i < 16 - NV:
+            k_acc = run("s", lambda: S.activation(row, row, F.Copy, accum_out=T.acc[:, i:i + 1]), k, k_ext)
+        else:
+            k_cv.append((i, k))
+    for j in range(NV):
+        i, k = k_cv[j]
+        k_cv[j] = run("v", lambda: V.tensor_tensor_scan(T.cv[:, j, 0:257], T.ones[:, 0:257], T.cmp[:, i, 0:257], 0.0, A.mult, A.add), k, k_ext, c_one)
+    k_rku = [cp("v", T.rku[:, 16 - NV:16], T.cv[:, :, 256], k_cv), cp("v", T.rku[:, 0:16 - NV], T.acc[:, 0:16 - NV], k_acc)]
 
     def spread(C, O, w, kc, pk, qs):
         ks = []
@@ -163,25 +172,21 @@ def rank_program(g, core, T, topo):
         return ks2
 
     def lists(W, W2, VT, C, O, kw, flip, pk, qs):
-        ks = []
-        n = 0
-        for m in range(3):
-            for h in range(2):
-                ks.append(cp(qs[n % len(qs)], W2[:, 32 * m + 16 * h:32 * m + 16 * h + 16], W[:, 16 * m:16 * m + 16], kw))
-                n += 1
-        kt = run("v", lambda: V.transpose(VT[:, :], W2[:, :]), ks)
+        ks = [cp(qs[h % len(qs)], W2[:, :, 16 * h:16 * h + 16], W[:, 0:CK], kw) for h in range(2)]
+        kt = run("v", lambda: V.transpose(VT[:, :], W2[:, :, :]), ks)
         kc = [cp(qs[e % len(qs)], C[:, 3 * (e ^ flip):3 * (e ^ flip) + 3], VT[:, 16 * e:96:32], kt) for e in range(2)]
         return spread(C, O, 3, kc, pk, qs)
 
     k_wa = cp("v", T.wa[:, 0:256].indirect(T.rku[:, 0:16]), T.val[:, :], k_rku, i_val)
     k_oa = lists(T.wa, T.wb, T.va, T.ca, T.oa, k_wa, (rank & 1) ^ 1, (rank >> 1) ^ 3, "vs")
-    k_of = [ts(T["of%d" % t][:, :], T.oa[:, :], float(t), A.add, k_oa) for t in (2, 0, 3, 1)]
-    k_of = {2: k_of[0], 0: k_of[1], 3: k_of[2], 1: k_of[3]}
+    k_of = cp("v", T.of[:, :], T.oa[:, :], k_oa)
+    win = [T.xs[:, :]] + [T["xs%d" % t][:, 16:16 + 4 * TOK - 3] for t in range(1, 4)]
     k_q1 = []
     for c in range(2):
         ks = []
         for t in (2, 0, 3, 1):
-            ks.append(cp("vs"[t // 2], T.xt[:, 4 * HALF * c + t:4 * HALF * (c + 1):4], T.xs[:, :].indirect(T["of%d" % t][:, 12 * c:12 * c + 12]), k_of[t], ("dx", 16)))
+            ks.append(cp("vs"[t // 2], T.xt[:, 4 * HALF * c + t:4 * HALF * (c + 1):4], win[t].indirect(T.of[:, 12 * c:12 * c + 12]), k_of,
+                         ("dxs", 48) if t else ("dx", 16)))
         o = HALF * c
         k_q1.append(run("v", lambda: V.quantize_mx(T.sb[:, o:o + HALF], T.ss[:, o:o + HALF], T.xt[:, 4 * o:4 * o + 4 * HALF]), ks))
 
@@ -215,16 +220,18 @@ def rank_program(g, core, T, topo):
 
     k_qw = run("v", lambda: V.quantize_mx(T.qw[:, :], T.sw[:, :], T.w1s[:, :]), ("dw1", 16))
     k_qe = run("v", lambda: V.quantize_mx(T.qe[:, :], T.se[:, :], T.em[:, :]), i_em)
-    k = cp("s", T.d2[:, 16:32], T.d2[:, 0:16], k_rk)
+    c_bp = run("v", lambda: V.tensor_scalar(T.bp[:, 0:1], T.bf[:, 2:3], float(B4), float(B4), A.mult, A.add), c_bf)
+    k_rk = [cp("v", T.acc[:, 16 - NV:16], T.cv[:, :, 256], k_cv), k_acc]
+    k_tk = ts(T.tk[:, :], T.acc[:, :], float(CK), A.is_lt, k_rk)
+    k_pb = ts(T.pb[:, :], T.acc[:, :], T.bp[:, 0:1], A.add, c_bp)
+    k = [tt(T.d2[:, 16 * h:16 * h + 16], T.tk[:, :], T.pb[:, :], A.mult, k_tk, k_pb) for h in range(2)]
     k = run("v", lambda: V.transpose(T.x1[:, :], T.d2[:, :]), k)
     ks = [cp("vs"[h], T.yb[:, 32 * h + 16 * j:32 * h + 16 * j + 16], T.x1[:, 16 * h:16 * h + 16], k) for h in range(2) for j in range(2)]
     k = run("v", lambda: V.transpose(T.x2[:, :], T.yb[:, :]), ks)
     ks = [cp("vs"[h], T.c2[:, 16 * h:16 * h + 16], T.x2[:, 32 * h:32 * h + 16], k) for h in range(2)]
-    ks = spread(T.c2, T.rka, 16, ks, 0, "vs")
-    k_tk = ts(T.tk[:, :], T.rka[:, :], float(CK), A.is_lt, ks)
-    k_pb = tt(T.pb[:, :], T.rka[:, :], T.base[:, :], A.add, i_base)
-    k_gm = ts(T.gm[:, :], T.eix[:, :], T.bf[:, 8:9], A.is_lt, i_eix, fg)
-    k_tp = tt(T.tp[:, :], T.tk[:, :], T.pb[:, :], A.mult, k_tk, k_pb)
+    k_tp = spread(T.c2, T.tp, 16, ks, 0, "vs")
+    c_pp = run("v", lambda: V.memset(T.pp[:, 0:B4], 0.0))
+    k_gm = ts(T.gm[:, :], T.eix[:, :], T.bf[:, 2:3], A.is_lt, i_eix, c_bf)
     k_km = tt(T.km[:, :], T.tp[:, :], T.gm[:, :], A.mult, k_tp, k_gm)
     kl1 = tt(T.l1[:, :], T.tp[:, 0:64], T.tp[:, 64:128], A.max, k_tp)
     kk1 = tt(T.k1[:, :], T.km[:, 0:64], T.km[:, 64:128], A.max, k_km)
@@ -286,28 +293,26 @@ def rank_program(g, core, T, topo):
                                arr2[c], k_qe, rb_free[bank], k_q2[1] if c else None)
     done = {}
     nxt = [0]
-    k_p = {-1: c_pp}
+    k_p = {}
+    blk = lambda e: e ^ rank ^ 7
     for c in range(2):
-        exps = sorted(e for e in range(N) if (e ^ rank ^ 7) // 4 == c)
+        exps = sorted(e for e in range(N) if blk(e) // 4 == c)
+        ks, k0 = [], []
+        for b in range(4):
+            q = "sv"[b % 2]
+            o = 512 * (4 * c + b)
+            if 0 in exps:
+                k0.append(cp(q, T.pp[:, B4 + CK * b:B4 + CK * b + CK], T.ps[:, o + CK * (blk(0) % 4):o + CK * (blk(0) % 4) + CK], k_d[(c, b)]))
+            ks.append(cp(q, T.vv[:, 4 * c:4 * c + 4, CK * b:CK * b + CK], T.ps[:, o:o + HALF], k_d[(c, b)]))
         for e in exps:
-            d = (e ^ rank ^ 7) % 4
-            ks = []
-            for b in (1, 0, 2, 3):
-                q = "s" if b else "v"
-                if c == 0 and b == 1:
-                    q = "v"
-                bank = 4 * c + b
-                src = T.ps[:, 512 * bank + CK * d:512 * bank + CK * d + CK]
-                dst = T.vv[:, B4 * e + CK * b:B4 * e + CK * b + CK] if e else T.pp[:, B4 + CK * b:B4 + CK * b + CK]
-                ks.append(cp(q, dst, src, k_d[(c, b)]))
-            done[e] = ks
+            done[e] = ks + k0
         while nxt[0] in done:
             e = nxt[0]
             if e == 0:
                 k_p[0] = done[0]
             else:
                 k_p[e] = run("v", lambda: V.tensor_tensor(T.pp[:, B4 * (e + 1):B4 * (e + 2)], T.pp[:, 0:B4 * (e + 1)].indirect(T.po[:, 12 * e:12 * e + 12]),
-                                                          T.vv[:, B4 * e:B4 * e + B4], A.add), k_p[e - 1], done[e], k_po, c_pp)
+                                                          T.vv[:, blk(e), :], A.add), k_p[e - 1], done[e], k_po, c_pp)
             nxt[0] += 1
     ny = 0
     for h in range(2):

@@ -2,11 +2,11 @@ from concourse.bass import DstId, RemoteDMATransfer
 from concourse.mybir import dt, AluOpType as A, AxisListType, ActivationFunctionType as F
 
 N, TOK, CK = 8, 256, 48
-B4 = 4 * CK
+B4, B2 = 4 * CK, 2 * CK
 OWN = (N - 1) * CK
 ALLC = (2 * N - 1) * CK
 HALF = 4 * CK
-NV = 2
+NE, NV = 3, 3
 ULP = 2.0 ** -24 * (1 + 2.0 ** -6)
 TINY = 2.0 ** -124
 
@@ -29,7 +29,7 @@ SCRATCH = {
     "wgo": ("sbuf", [128, 32], "int32"), "wgu": ("sbuf", [128, 32], "uint16"),
     "col": ("sbuf", [128, 256], "float32"), "val": ("sbuf", [128, TOK], "float32"),
     "meq": ("sbuf", [128, 256], "float32"), "mne": ("sbuf", [128, 256], "float32"), "mnb": ("sbuf", [128, 256], "bfloat16"),
-    "idw": ("sbuf", [128, 9 * B4], "float32"),
+    "idw": ("sbuf", [128, 9 * B2], "float32"),
     "eix": ("sbuf", [128, 128], "float32"), "gm": ("sbuf", [128, 128], "float32"),
     "m1": ("sbuf", [128, 256], "float32"), "fs": ("sbuf", [128, 256], "float32"),
     "ulp": ("sbuf", [128, 256], "float32"), "zz": ("sbuf", [128, 512], "float32"),
@@ -51,8 +51,9 @@ SCRATCH = {
     "k4": ("sbuf", [128, 16], "float32"),
     "row": ("sbuf", [128, 256], "float32"), "wc": ("sbuf", [128, 256], "float32"), "wd": ("sbuf", [128, 3, 32], "float32"),
     "vc": ("sbuf", [128, 96], "float32"), "cc": ("sbuf", [128, 6], "float32"), "oc": ("sbuf", [128, 24], "float32"),
-    "po": ("sbuf", [128, 96], "uint16"), "lb": ("sbuf", [128, 64], "uint16"),
-    "vv": ("sbuf", [128, N, B4], "float32"), "pp": ("sbuf", [128, (N + 1) * B4], "float32"),
+    "po": ("sbuf", [128, 48], "uint16"), "lb": ("sbuf", [128, 32], "uint16"),
+    "vv": ("sbuf", [128, N, B4], "float32"),
+    "pp0": ("sbuf", [128, (N + 1) * B2], "float32"), "pp1": ("sbuf", [128, (N + 1) * B2], "float32"),
     "yo": ("sbuf", [128, 4 * TOK], "float32"),
 }
 SEMAPHORES = ["v", "s", "t", "p", "dwg", "dx", "dxs", "dw1", "dy", "a1A", "a1B", "a2A", "a2B", "loc"]
@@ -113,7 +114,7 @@ def rank_program(g, core, T, topo):
     for b in range(4):
         i_em = run("p", lambda: g.affine_select(T.em[:, 512 * b:512 * b + 512], T.ones[:, :], [[-1, 512]], A.is_equal, 0.0, b, 4), c_one)
     i_eix = run("p", lambda: g.iota(T.eix[:, :], [[1, 8], [0, 16]], 0, 0, allow_small_or_imprecise_dtypes=True))
-    i_idw = run("p", lambda: g.iota(T.idw[:, :], [[1, 9 * B4]], 0, 0, allow_small_or_imprecise_dtypes=True))
+    i_idw = run("p", lambda: g.iota(T.idw[:, :], [[1, 9 * B2]], 0, 0, allow_small_or_imprecise_dtypes=True))
 
     cb = [ts(T.bi[:, 0:1], T.pi[:, 0:1], 3, A.bitwise_and, i_pi),
           ts(T.bi[:, 1:2], T.pi[:, 0:1], 15, A.bitwise_and, i_pi),
@@ -135,26 +136,33 @@ def rank_program(g, core, T, topo):
     k_ulp = run("s", lambda: S.activation(T.ulp[:, :], Z2, F.Abs, bias=TINY, scale=ULP), k_z2)
     k_zc = cp("s", T.zz[:, 0:256], Z2, k_z2)
     k_m1 = tt(T.m1[:, :], Z, T.meq[:, :], A.mult, k_z, c_meq)
-    k_fs = run("v", lambda: V.tensor_tensor_scan(T.fs[:, :], T.mne[:, :], T.m1[:, :], 0.0, A.mult, A.add), k_m1, c_mne)
     k_zn = tt(T.zz[:, 256:512], Z, T.ulp[:, :], A.add, k_ulp)
-    k_eq = tt(T.eq[:, :], Z, T.fs[:, :], A.is_equal, k_fs)
-    k_eqs = run("v", lambda: V.tensor_tensor_scan(T.eqs[:, :], T.mnb[:, :], T.eq[:, :], 0.0, A.mult, A.subtract), k_eq, c_mnb)
-    k_ext = None
-    k_acc = None
+    k_fs = run("v", lambda: V.tensor_tensor_scan(T.fs[:, :], T.mne[:, :], T.m1[:, :], 0.0, A.mult, A.add), k_m1, c_mne)
+    k_eqs, k_ext, k_acc, k_fix = None, None, None, None
     k_cv = []
     for i in range(16):
         own = T.fs[:, 16 * i + 15:16 * i + 16]
-        k = ts(T.cmp[:, i, 0:256], T.zz[:, 16 * i + 16:16 * i + 272], own, A.is_gt, k_zc, k_zn)
-        if i == 0:
-            k_ext = cp("v", T.cmp[:, :, 256], T.eqs[:, 15:256:16], k_eqs)
-        row = T.cmp[:, i, 0:257]
-        if i < 16 - NV:
+        k = ts(T.cmp[:, i, 0:256], T.zz[:, 16 * i + 16:16 * i + 272], own, A.is_gt, k_fs, k_zc, k_zn)
+        if i < NE:
+            row = T.cmp[:, i, 0:256]
+            k_acc = run("s", lambda: S.activation(row, row, F.Copy, accum_out=T.acc[:, i:i + 1]), k)
+            k_fix = k_acc
+        elif i < 16 - NV:
+            row = T.cmp[:, i, 0:257]
             k_acc = run("s", lambda: S.activation(row, row, F.Copy, accum_out=T.acc[:, i:i + 1]), k, k_ext)
         else:
             k_cv.append((i, k))
+        if i == NE - 2:
+            k_eq = tt(T.eq[:, :], Z, T.fs[:, :], A.is_equal, k_fs)
+        if i == NE - 1:
+            k_eqs = run("v", lambda: V.tensor_tensor_scan(T.eqs[:, :], T.mnb[:, :], T.eq[:, :], 0.0, A.mult, A.subtract), k_eq, c_mnb)
+            k_ext = cp("v", T.cmp[:, NE:16, 256], T.eqs[:, 16 * NE + 15:256:16], k_eqs)
+        if i == NE + 4:
+            k_fix = tt(T.acc[:, 0:NE], T.acc[:, 0:NE], T.eqs[:, 15:16 * NE:16], A.add, k_fix, k_eqs)
     for j in range(NV):
         i, k = k_cv[j]
         k_cv[j] = run("v", lambda: V.tensor_tensor_scan(T.cv[:, j, 0:257], T.ones[:, 0:257], T.cmp[:, i, 0:257], 0.0, A.mult, A.add), k, k_ext, c_one)
+    k_acc = [k_acc, k_fix]
     k_rku = [cp("v", T.rku[:, 16 - NV:16], T.cv[:, :, 256], k_cv), cp("v", T.rku[:, 0:16 - NV], T.acc[:, 0:16 - NV], k_acc)]
 
     def spread(C, O, w, kc, pk, qs):
@@ -220,8 +228,8 @@ def rank_program(g, core, T, topo):
 
     k_qw = run("v", lambda: V.quantize_mx(T.qw[:, :], T.sw[:, :], T.w1s[:, :]), ("dw1", 16))
     k_qe = run("v", lambda: V.quantize_mx(T.qe[:, :], T.se[:, :], T.em[:, :]), i_em)
-    c_bp = run("v", lambda: V.tensor_scalar(T.bp[:, 0:1], T.bf[:, 2:3], float(B4), float(B4), A.mult, A.add), c_bf)
-    k_rk = [cp("v", T.acc[:, 16 - NV:16], T.cv[:, :, 256], k_cv), k_acc]
+    c_bp = run("v", lambda: V.tensor_scalar(T.bp[:, 0:1], T.bf[:, 2:3], float(B2), float(B2), A.mult, A.add), c_bf)
+    k_rk = [cp("v", T.acc[:, 16 - NV:16], T.cv[:, :, 256], k_cv)] + k_acc
     k_tk = ts(T.tk[:, :], T.acc[:, :], float(CK), A.is_lt, k_rk)
     k_pb = ts(T.pb[:, :], T.acc[:, :], T.bp[:, 0:1], A.add, c_bp)
     k = [tt(T.d2[:, 16 * h:16 * h + 16], T.tk[:, :], T.pb[:, :], A.mult, k_tk, k_pb) for h in range(2)]
@@ -230,7 +238,7 @@ def rank_program(g, core, T, topo):
     k = run("v", lambda: V.transpose(T.x2[:, :], T.yb[:, :]), ks)
     ks = [cp("vs"[h], T.c2[:, 16 * h:16 * h + 16], T.x2[:, 32 * h:32 * h + 16], k) for h in range(2)]
     k_tp = spread(T.c2, T.tp, 16, ks, 0, "vs")
-    c_pp = run("v", lambda: V.memset(T.pp[:, 0:B4], 0.0))
+    c_pp = [run("v", lambda: V.memset(T["pp%d" % h][:, 0:B2], 0.0)) for h in range(2)]
     k_gm = ts(T.gm[:, :], T.eix[:, :], T.bf[:, 2:3], A.is_lt, i_eix, c_bf)
     k_km = tt(T.km[:, :], T.tp[:, :], T.gm[:, :], A.mult, k_tp, k_gm)
     kl1 = tt(T.l1[:, :], T.tp[:, 0:64], T.tp[:, 64:128], A.max, k_tp)
@@ -240,7 +248,7 @@ def rank_program(g, core, T, topo):
     kl3 = tt(T.l3[:, :], T.l2[:, 0:16], T.l2[:, 16:32], A.max, kl2)
     kk3 = tt(T.k4[:, :], T.k2[:, 0:16], T.k2[:, 16:32], A.max, kk2)
     kk4 = cp("v", T.k3[:, :], T.k4[:, :], kk3)
-    k_lb = [ts(T.lb[:, 16 * b:16 * b + 16], T.l3[:, :], float(CK * b), A.add, kl3) for b in range(4)]
+    k_lb = [ts(T.lb[:, 16 * b:16 * b + 16], T.l3[:, :], float(CK * b), A.add, kl3) for b in range(2)]
 
     out2, in2 = (lambda de: OWN + CK * de), (lambda de: CK * (7 - de))
     arr1 = [("a1A", nA), ("a1B", nB)]
@@ -279,9 +287,9 @@ def rank_program(g, core, T, topo):
     k_wc = cp("v", T.wc[:, 0:256].indirect(T.rku[:, 0:16]), T.row[:, :], k)
     k_oc = lists(T.wc, T.wd, T.vc, T.cc, T.oc, k_wc, 0, 0, "vs")
     k_po = None
-    for b in range(4):
+    for b in range(2):
         for m in range(3):
-            k_po = ts(T.po[:, 3 * b + m:96:12], T.oc[:, m:24:3], float(CK * b), A.add, k_oc)
+            k_po = ts(T.po[:, 3 * b + m:48:6], T.oc[:, m:24:3], float(CK * b), A.add, k_oc)
 
     arr2 = [("a2A", mA), ("a2B", mB)]
     k_d = {}
@@ -302,23 +310,27 @@ def rank_program(g, core, T, topo):
             q = "sv"[b % 2]
             o = 512 * (4 * c + b)
             if 0 in exps:
-                k0.append(cp(q, T.pp[:, B4 + CK * b:B4 + CK * b + CK], T.ps[:, o + CK * (blk(0) % 4):o + CK * (blk(0) % 4) + CK], k_d[(c, b)]))
+                p = B2 + CK * (b % 2)
+                k0.append(cp(q, T["pp%d" % (b // 2)][:, p:p + CK], T.ps[:, o + CK * (blk(0) % 4):o + CK * (blk(0) % 4) + CK], k_d[(c, b)]))
             ks.append(cp(q, T.vv[:, 4 * c:4 * c + 4, CK * b:CK * b + CK], T.ps[:, o:o + HALF], k_d[(c, b)]))
         for e in exps:
-            done[e] = ks + k0
+            done[e] = [ks[0:2] + k0[0:2], ks[2:4] + k0[2:4]]
         while nxt[0] in done:
             e = nxt[0]
-            if e == 0:
-                k_p[0] = done[0]
-            else:
-                k_p[e] = run("v", lambda: V.tensor_tensor(T.pp[:, B4 * (e + 1):B4 * (e + 2)], T.pp[:, 0:B4 * (e + 1)].indirect(T.po[:, 12 * e:12 * e + 12]),
-                                                          T.vv[:, blk(e), :], A.add), k_p[e - 1], done[e], k_po, c_pp)
+            for h in range(2):
+                P = T["pp%d" % h]
+                if e == 0:
+                    k_p[(0, h)] = done[0][h]
+                else:
+                    k_p[(e, h)] = run("v", lambda: V.tensor_tensor(P[:, B2 * (e + 1):B2 * (e + 2)], P[:, 0:B2 * (e + 1)].indirect(T.po[:, 6 * e:6 * e + 6]),
+                                                                   T.vv[:, blk(e), B2 * h:B2 * h + B2], A.add), k_p[(e - 1, h)], done[e][h], k_po, c_pp)
             nxt[0] += 1
     ny = 0
     for h in range(2):
         ks = []
-        for b in (2, 0, 3, 1):
-            ks.append(cp("vs"[b // 2], T.yo[:, 512 * h + b:512 * (h + 1):4], T.pp[:, :].indirect(T.lb[:, 16 * b + 8 * h:16 * b + 8 * h + 8]), k_p[7], k_lb[b]))
+        for b in (0, 2, 1, 3):
+            ks.append(cp("sv"[b // 2], T.yo[:, 512 * h + b:512 * (h + 1):4], T["pp%d" % (b // 2)][:, :].indirect(T.lb[:, 16 * (b % 2) + 8 * h:16 * (b % 2) + 8 * h + 8]),
+                         k_p[(7, b // 2)], k_lb[b % 2]))
         need("y", ks)
         g.sync.dma_start(T.y[:, 512 * h:512 * h + 512], T.yo[:, 512 * h:512 * h + 512]).then_inc(T.sem.dy, 16)
         ny += 16

from concourse.bass import DstId, RemoteDMATransfer
from concourse.mybir import dt, AluOpType as A, AxisListType, ActivationFunctionType as F

N, TOK, CK = 8, 256, 48
B4, B2 = 4 * CK, 2 * CK
OWN = (N - 1) * CK
ALLC = (2 * N - 1) * CK
HALF = 4 * CK
NE, NV = 3, 3
ULP = 2.0 ** -24 * (1 + 2.0 ** -6)
TINY = 2.0 ** -124

SCRATCH = {
    "xs": ("sbuf", [128, 4 * TOK], "bfloat16"),
    "xs1": ("sbuf", [128, 4 * TOK + 16], "bfloat16"), "xs2": ("sbuf", [128, 4 * TOK + 16], "bfloat16"),
    "xs3": ("sbuf", [128, 4 * TOK + 16], "bfloat16"),
    "wgs": ("sbuf", [128, 32], "bfloat16"),
    "wr": ("sbuf", [128, 512], "bfloat16"),
    "w1s": ("sbuf", [128, 2048], "bfloat16"),
    "qx": ("sbuf", [128, TOK], "float8_e4m3fn_x4"), "sx": ("sbuf", [128, TOK], "uint8"),
    "qr": ("sbuf", [128, 128], "float8_e4m3fn_x4"), "sr": ("sbuf", [128, 128], "uint8"),
    "qw": ("sbuf", [128, 512], "float8_e4m3fn_x4"), "sw": ("sbuf", [128, 512], "uint8"),
    "ones": ("sbuf", [128, 512], "bfloat16"),
    "em": ("sbuf", [128, 2048], "bfloat16"),
    "qe": ("sbuf", [128, 512], "float8_e4m3fn_x4"), "se": ("sbuf", [128, 512], "uint8"),
    "ps": ("psum", [128, 4096], "float32"),
    "pi": ("sbuf", [128, 4], "int32"), "bi": ("sbuf", [128, 4], "int32"), "bf": ("sbuf", [128, 4], "float32"),
    "bp": ("sbuf", [128, 4], "float32"),
    "wgo": ("sbuf", [128, 32], "int32"), "wgu": ("sbuf", [128, 32], "uint16"),
    "col": ("sbuf", [128, 256], "float32"), "val": ("sbuf", [128, TOK], "float32"),
    "meq": ("sbuf", [128, 256], "float32"), "mne": ("sbuf", [128, 256], "float32"), "mnb": ("sbuf", [128, 256], "bfloat16"),
    "idw": ("sbuf", [128, 9 * B2], "float32"),
    "eix": ("sbuf", [128, 128], "float32"), "gm": ("sbuf", [128, 128], "float32"),
    "m1": ("sbuf", [128, 256], "float32"), "fs": ("sbuf", [128, 256], "float32"),
    "ulp": ("sbuf", [128, 256], "float32"), "zz": ("sbuf", [128, 512], "float32"),
    "eq": ("sbuf", [128, 256], "bfloat16"), "eqs": ("sbuf", [128, 256], "bfloat16"),
    "cmp": ("sbuf", [128, 16, 264], "bfloat16"), "cv": ("sbuf", [128, NV, 264], "bfloat16"), "acc": ("sbuf", [128, 16], "float32"),
    "rku": ("sbuf", [128, 16], "uint16"),
    "wa": ("sbuf", [128, 256], "float32"), "wb": ("sbuf", [128, 3, 32], "float32"), "va": ("sbuf", [128, 96], "float32"),
    "ca": ("sbuf", [128, 6], "float32"), "oa": ("sbuf", [128, 24], "float32"), "of": ("sbuf", [128, 24], "uint16"),
    "xt": ("sbuf", [128, 4 * N * CK], "bfloat16"),
    "sb": ("sbuf", [128, ALLC], "float8_e4m3fn_x4"), "ss": ("sbuf", [128, ALLC], "uint8"),
    "ht": ("sbuf", [128, 4 * N * CK], "bfloat16"),
    "rb": ("sbuf", [128, ALLC], "float8_e4m3fn_x4"), "rs": ("sbuf", [128, ALLC], "uint8"),
    "tk": ("sbuf", [128, 16], "float32"), "pb": ("sbuf", [128, 16], "float32"), "d2": ("sbuf", [128, 32], "float32"),
    "x1": ("sbuf", [128, 32], "float32"), "yb": ("sbuf", [128, 64], "float32"), "x2": ("sbuf", [128, 64], "float32"),
    "c2": ("sbuf", [128, 32], "float32"), "tp": ("sbuf", [128, 128], "float32"),
    "km": ("sbuf", [128, 128], "float32"),
    "l1": ("sbuf", [128, 64], "float32"), "l2": ("sbuf", [128, 32], "float32"), "l3": ("sbuf", [128, 16], "float32"),
    "k1": ("sbuf", [128, 64], "float32"), "k2": ("sbuf", [128, 32], "float32"), "k3": ("sbuf", [128, 16], "uint16"),
    "k4": ("sbuf", [128, 16], "float32"),
    "row": ("sbuf", [128, 256], "float32"), "wc": ("sbuf", [128, 256], "float32"), "wd": ("sbuf", [128, 3, 32], "float32"),
    "vc": ("sbuf", [128, 96], "float32"), "cc": ("sbuf", [128, 6], "float32"), "oc": ("sbuf", [128, 24], "float32"),
    "po": ("sbuf", [128, 48], "uint16"), "lb": ("sbuf", [128, 32], "uint16"),
    "vv": ("sbuf", [128, N, B4], "float32"),
    "pp0": ("sbuf", [128, (N + 1) * B2], "float32"), "pp1": ("sbuf", [128, (N + 1) * B2], "float32"),
    "yo": ("sbuf", [128, 4 * TOK], "float32"),
}
SEMAPHORES = ["v", "s", "t", "p", "dwg", "dx", "dxs", "dw1", "dy", "a1A", "a1B", "a2A", "a2B", "loc"]


def rank_program(g, core, T, topo):
    rank = T.rank_of(core)
    if rank is None:
        return
    Q = {"v": g.vector, "s": g.scalar, "t": g.tensor, "p": g, "y": g.sync}
    cnt = {"v": 0, "s": 0, "t": 0, "p": 0}
    known = {}

    def need(q, *deps):
        best = {}
        for d in deps:
            if d is None:
                continue
            for sem, val in (d if isinstance(d, list) else [d]):
                best[sem] = max(best.get(sem, 0), val)
        for sem, val in best.items():
            if known.get((q, sem), 0) < val:
                Q[q].wait_ge(T.sem[sem], val)
                known[(q, sem)] = val

    def run(q, fn, *deps):
        need(q, *deps)
        cnt[q] += 1
        fn().then_inc(T.sem[q], 1)
        return (q, cnt[q])

    V, S = g.vector, g.scalar

    def cp(q, out, in_, *deps):
        if q == "v":
            return run("v", lambda: V.tensor_copy(out, in_), *deps)
        return run("s", lambda: S.activation(out, in_, F.Copy), *deps)

    def ts(out, in0, s1, op0, *deps):
        return run("v", lambda: V.tensor_scalar(out, in0, s1, None, op0), *deps)

    def tt(out, a, b, op, *deps):
        return run("v", lambda: V.tensor_tensor(out, a, b, op), *deps)

    g.sync.dma_start(T.xs[:, :], T.x[:, :]).then_inc(T.sem.dx, 16)
    g.scalar.dma_start(T.wgs[:, 0:32], T.wg[:, 0:32]).then_inc(T.sem.dwg, 16)
    g.sync.wait_ge(T.sem.dx, 16)
    for t in range(1, 4):
        g.sync.dma_start(T["xs%d" % t][:, 16 - t:16 - t + 4 * TOK], T.x[:, :]).then_inc(T.sem.dxs, 16)
    g.sync.dma_start(T.w1s[:, :], T.w1[:, :]).then_inc(T.sem.dw1, 16)

    i_pi = run("p", lambda: g.iota(T.pi[:, 0:1], [[0, 1]], 0, 1))
    i_wgo = run("p", lambda: g.iota(T.wgo[:, :], [[4, 8], [0, 4]], 0, 0))
    i_col = run("p", lambda: g.iota(T.col[:, :], [[0, 16], [1, 16]], 0, 0, allow_small_or_imprecise_dtypes=True))
    i_val = run("p", lambda: g.iota(T.val[:, :], [[4, TOK]], 0, 0, allow_small_or_imprecise_dtypes=True))
    c_one = run("v", lambda: V.memset(T.ones[:, :], 1.0))
    i_em = None
    for b in range(4):
        i_em = run("p", lambda: g.affine_select(T.em[:, 512 * b:512 * b + 512], T.ones[:, :], [[-1, 512]], A.is_equal, 0.0, b, 4), c_one)
    i_eix = run("p", lambda: g.iota(T.eix[:, :], [[1, 8], [0, 16]], 0, 0, allow_small_or_imprecise_dtypes=True))
    i_idw = run("p", lambda: g.iota(T.idw[:, :], [[1, 9 * B2]], 0, 0, allow_small_or_imprecise_dtypes=True))

    cb = [ts(T.bi[:, 0:1], T.pi[:, 0:1], 3, A.bitwise_and, i_pi),
          ts(T.bi[:, 1:2], T.pi[:, 0:1], 15, A.bitwise_and, i_pi),
          ts(T.bi[:, 2:3], T.pi[:, 0:1], 4, A.arith_shift_right, i_pi)]
    c_bf = cp("v", T.bf[:, 0:3], T.bi[:, 0:3], cb)
    c_wgu = ts(T.wgu[:, :], T.wgo[:, :], T.bf[:, 0:1], A.add, i_wgo, c_bf)
    R = T.bf[:, 1:2]
    c_meq = ts(T.meq[:, :], T.col[:, :], R, A.is_equal, i_col, c_bf)
    c_mne = ts(T.mne[:, :], T.col[:, :], R, A.not_equal)

    k_wr = cp("s", T.wr[:, :], T.wgs[:, 0:32].indirect(T.wgu[:, 0:32]), ("dwg", 16), c_wgu)
    k_qr = run("v", lambda: V.quantize_mx(T.qr[:, :], T.sr[:, :], T.wr[:, :]), k_wr)
    k_qx = run("v", lambda: V.quantize_mx(T.qx[:, :], T.sx[:, :], T.xs[:, :]), ("dx", 16))
    Z, Z2 = T.ps[:, 3584:3584 + TOK], T.ps[:, 3072:3072 + TOK]
    k_z2 = run("t", lambda: g.tensor.matmul_mx(Z2, T.qr[:, :], T.sr[:, :], T.qx[:, :], T.sx[:, :], True, True), k_qr, k_qx)
    k_z = run("t", lambda: g.tensor.matmul_mx(Z, T.qr[:, :], T.sr[:, :], T.qx[:, :], T.sx[:, :], True, True), k_qr, k_qx)
    c_mnb = ts(T.mnb[:, :], T.col[:, :], R, A.not_equal)

    k_ulp = run("s", lambda: S.activation(T.ulp[:, :], Z2, F.Abs, bias=TINY, scale=ULP), k_z2)
    k_zc = cp("s", T.zz[:, 0:256], Z2, k_z2)
    k_m1 = tt(T.m1[:, :], Z, T.meq[:, :], A.mult, k_z, c_meq)
    k_zn = tt(T.zz[:, 256:512], Z, T.ulp[:, :], A.add, k_ulp)
    k_fs = run("v", lambda: V.tensor_tensor_scan(T.fs[:, :], T.mne[:, :], T.m1[:, :], 0.0, A.mult, A.add), k_m1, c_mne)
    k_eqs, k_ext, k_acc, k_fix = None, None, None, None
    k_cv = []
    for i in range(16):
        own = T.fs[:, 16 * i + 15:16 * i + 16]
        k = ts(T.cmp[:, i, 0:256], T.zz[:, 16 * i + 16:16 * i + 272], own, A.is_gt, k_fs, k_zc, k_zn)
        if i < NE:
            row = T.cmp[:, i, 0:256]
            k_acc = run("s", lambda: S.activation(row, row, F.Copy, accum_out=T.acc[:, i:i + 1]), k)
            k_fix = k_acc
        elif i < 16 - NV:
            row = T.cmp[:, i, 0:257]
            k_acc = run("s", lambda: S.activation(row, row, F.Copy, accum_out=T.acc[:, i:i + 1]), k, k_ext)
        else:
            k_cv.append((i, k))
        if i == NE - 2:
            k_eq = tt(T.eq[:, :], Z, T.fs[:, :], A.is_equal, k_fs)
        if i == NE - 1:
            k_eqs = run("v", lambda: V.tensor_tensor_scan(T.eqs[:, :], T.mnb[:, :], T.eq[:, :], 0.0, A.mult, A.subtract), k_eq, c_mnb)
            k_ext = cp("v", T.cmp[:, NE:16, 256], T.eqs[:, 16 * NE + 15:256:16], k_eqs)
        if i == NE + 4:
            k_fix = tt(T.acc[:, 0:NE], T.acc[:, 0:NE], T.eqs[:, 15:16 * NE:16], A.add, k_fix, k_eqs)
    for j in range(NV):
        i, k = k_cv[j]
        k_cv[j] = run("v", lambda: V.tensor_tensor_scan(T.cv[:, j, 0:257], T.ones[:, 0:257], T.cmp[:, i, 0:257], 0.0, A.mult, A.add), k, k_ext, c_one)
    k_acc = [k_acc, k_fix]
    k_rku = [cp("v", T.rku[:, 16 - NV:16], T.cv[:, :, 256], k_cv), cp("v", T.rku[:, 0:16 - NV], T.acc[:, 0:16 - NV], k_acc)]

    def spread(C, O, w, kc, pk, qs):
        ks = []
        n = 0
        for q in range(4):
            for d in (q, q ^ 1):
                o = 2 * w * (q ^ pk)
                ks.append(cp(qs[n % len(qs)], O[32 * d:32 * d + 32, o:o + 2 * w], C[32 * q:32 * q + 32, :], kc))
                n += 1
        ks2 = list(ks)
        for h in range(2):
            o = 4 * w * (h ^ (pk >> 1))
            ks2.append(cp(qs[h % len(qs)], O[64 * (1 - h):64 * (1 - h) + 64, o:o + 4 * w], O[64 * h:64 * h + 64, o:o + 4 * w], ks))
        return ks2

    def lists(W, W2, VT, C, O, kw, flip, pk, qs):
        ks = [cp(qs[h % len(qs)], W2[:, :, 16 * h:16 * h + 16], W[:, 0:CK], kw) for h in range(2)]
        kt = run("v", lambda: V.transpose(VT[:, :], W2[:, :, :]), ks)
        kc = [cp(qs[e % len(qs)], C[:, 3 * (e ^ flip):3 * (e ^ flip) + 3], VT[:, 16 * e:96:32], kt) for e in range(2)]
        return spread(C, O, 3, kc, pk, qs)

    k_wa = cp("v", T.wa[:, 0:256].indirect(T.rku[:, 0:16]), T.val[:, :], k_rku, i_val)
    k_oa = lists(T.wa, T.wb, T.va, T.ca, T.oa, k_wa, (rank & 1) ^ 1, (rank >> 1) ^ 3, "vs")
    k_of = cp("v", T.of[:, :], T.oa[:, :], k_oa)
    win = [T.xs[:, :]] + [T["xs%d" % t][:, 16:16 + 4 * TOK - 3] for t in range(1, 4)]
    k_q1 = []
    for c in range(2):
        ks = []
        for t in (2, 0, 3, 1):
            ks.append(cp("vs"[t // 2], T.xt[:, 4 * HALF * c + t:4 * HALF * (c + 1):4], win[t].indirect(T.of[:, 12 * c:12 * c + 12]), k_of,
                         ("dxs", 48) if t else ("dx", 16)))
        o = HALF * c
        k_q1.append(run("v", lambda: V.quantize_mx(T.sb[:, o:o + HALF], T.ss[:, o:o + HALF], T.xt[:, 4 * o:4 * o + 4 * HALF]), ks))

    loc = [0]

    def send(dels, src_col, dst_col, codes, plane, sem):
        per = 8 // (4 if len(dels) > 2 else len(dels))
        for view in ("q", "s"):
            tr = []
            for j, de in enumerate(dels):
                dst = T.cores[rank ^ de]
                eng = topo.engines(core, dst)
                mask = sum(1 << e for e in eng[j * per:(j + 1) * per])
                rid, pid = topo.addr(dst, core)
                a, b = src_col(de), dst_col(de)
                if view == "q":
                    sa, da = codes[:, a:a + CK].bitcast(dt.uint8), codes[:, b:b + CK].bitcast(dt.uint8)
                else:
                    sa, da = plane[:, a:a + CK], plane[:, b:b + CK]
                tr.append(RemoteDMATransfer(dst_ids=[DstId(rid=rid, pnc=pid)], dma_engine_mask=mask, remote_sem=T.sem[sem], src=sa, dst=da))
                loc[0] += per
            g.remote_dma_fused(tr, local_sem=T.sem.loc)
        return 2 * per * len(dels)

    FAR, NEAR = (7, 6, 5, 4), (3, 2, 1)
    out1, in1 = (lambda de: CK * (7 - de)), (lambda de: OWN + CK * de)
    need("p", k_q1[0])
    nA = send(FAR, out1, in1, T.sb, T.ss, "a1A")
    need("p", k_q1[1])
    nB = send(NEAR, out1, in1, T.sb, T.ss, "a1B")

    k_qw = run("v", lambda: V.quantize_mx(T.qw[:, :], T.sw[:, :], T.w1s[:, :]), ("dw1", 16))
    k_qe = run("v", lambda: V.quantize_mx(T.qe[:, :], T.se[:, :], T.em[:, :]), i_em)
    c_bp = run("v", lambda: V.tensor_scalar(T.bp[:, 0:1], T.bf[:, 2:3], float(B2), float(B2), A.mult, A.add), c_bf)
    k_rk = [cp("v", T.acc[:, 16 - NV:16], T.cv[:, :, 256], k_cv)] + k_acc
    k_tk = ts(T.tk[:, :], T.acc[:, :], float(CK), A.is_lt, k_rk)
    k_pb = ts(T.pb[:, :], T.acc[:, :], T.bp[:, 0:1], A.add, c_bp)
    k = [tt(T.d2[:, 16 * h:16 * h + 16], T.tk[:, :], T.pb[:, :], A.mult, k_tk, k_pb) for h in range(2)]
    k = run("v", lambda: V.transpose(T.x1[:, :], T.d2[:, :]), k)
    ks = [cp("vs"[h], T.yb[:, 32 * h + 16 * j:32 * h + 16 * j + 16], T.x1[:, 16 * h:16 * h + 16], k) for h in range(2) for j in range(2)]
    k = run("v", lambda: V.transpose(T.x2[:, :], T.yb[:, :]), ks)
    ks = [cp("vs"[h], T.c2[:, 16 * h:16 * h + 16], T.x2[:, 32 * h:32 * h + 16], k) for h in range(2)]
    k_tp = spread(T.c2, T.tp, 16, ks, 0, "vs")
    c_pp = [run("v", lambda: V.memset(T["pp%d" % h][:, 0:B2], 0.0)) for h in range(2)]
    k_gm = ts(T.gm[:, :], T.eix[:, :], T.bf[:, 2:3], A.is_lt, i_eix, c_bf)
    k_km = tt(T.km[:, :], T.tp[:, :], T.gm[:, :], A.mult, k_tp, k_gm)
    kl1 = tt(T.l1[:, :], T.tp[:, 0:64], T.tp[:, 64:128], A.max, k_tp)
    kk1 = tt(T.k1[:, :], T.km[:, 0:64], T.km[:, 64:128], A.max, k_km)
    kl2 = tt(T.l2[:, :], T.l1[:, 0:32], T.l1[:, 32:64], A.max, kl1)
    kk2 = tt(T.k2[:, :], T.k1[:, 0:32], T.k1[:, 32:64], A.max, kk1)
    kl3 = tt(T.l3[:, :], T.l2[:, 0:16], T.l2[:, 16:32], A.max, kl2)
    kk3 = tt(T.k4[:, :], T.k2[:, 0:16], T.k2[:, 16:32], A.max, kk2)
    kk4 = cp("v", T.k3[:, :], T.k4[:, :], kk3)
    k_lb = [ts(T.lb[:, 16 * b:16 * b + 16], T.l3[:, :], float(CK * b), A.add, kl3) for b in range(2)]

    out2, in2 = (lambda de: OWN + CK * de), (lambda de: CK * (7 - de))
    arr1 = [("a1A", nA), ("a1B", nB)]
    rb_free = {}
    k_r = {}
    for c in range(2):
        col = OWN + HALF * (1 - c)
        for i in range(4):
            bank = 4 * c + i
            k_r[(c, i)] = run("t", lambda: g.tensor.matmul_mx(T.ps[:, 512 * bank:512 * bank + HALF], T.qw[:, 128 * i:128 * i + 128], T.sw[:, 128 * i:128 * i + 128],
                                                  T.sb[:, col:col + HALF], T.ss[:, col:col + HALF], True, True),
                               arr1[c], k_qw, k_q1[1] if c else None, k_rku)
    k_q2 = []
    for c in range(2):
        o = 4 * HALF * (1 - c)
        ks = []
        for i in range(4):
            bank = 4 * c + i
            out, src = T.ht[:, o + i:o + 4 * HALF:4], T.ps[:, 512 * bank:512 * bank + HALF]
            if i % 2 == 0:
                kk = run("s", lambda: S.activation(out, src, F.Relu, scale=0.05), k_r[(c, i)])
            else:
                kk = run("v", lambda: V.tensor_scalar(out, src, 0.0, 0.05, A.max, A.mult), k_r[(c, i)])
            ks.append(kk)
            rb_free[bank] = kk
        col = OWN + HALF * (1 - c)
        k_q2.append(run("v", lambda: V.quantize_mx(T.rb[:, col:col + HALF], T.rs[:, col:col + HALF], T.ht[:, o:o + 4 * HALF]), ks))
        need("p", k_q2[c])
        n2 = send((FAR, NEAR)[c], out2, in2, T.rb, T.rs, ("a2A", "a2B")[c])
        if c == 0:
            mA = n2
        else:
            mB = n2

    k = cp("v", T.row[:, :], T.idw[:, :].indirect(T.k3[:, 0:16]), kk4, i_idw)
    k_wc = cp("v", T.wc[:, 0:256].indirect(T.rku[:, 0:16]), T.row[:, :], k)
    k_oc = lists(T.wc, T.wd, T.vc, T.cc, T.oc, k_wc, 0, 0, "vs")
    k_po = None
    for b in range(2):
        for m in range(3):
            k_po = ts(T.po[:, 3 * b + m:48:6], T.oc[:, m:24:3], float(CK * b), A.add, k_oc)

    arr2 = [("a2A", mA), ("a2B", mB)]
    k_d = {}
    for c in range(2):
        for b in range(4):
            bank = 4 * c + b
            k_d[(c, b)] = run("t", lambda: g.tensor.matmul_mx(T.ps[:, 512 * bank:512 * bank + HALF], T.qe[:, 128 * b:128 * b + 128], T.se[:, 128 * b:128 * b + 128],
                                                  T.rb[:, HALF * c:HALF * c + HALF], T.rs[:, HALF * c:HALF * c + HALF], True, True),
                               arr2[c], k_qe, rb_free[bank], k_q2[1] if c else None)
    done = {}
    nxt = [0]
    k_p = {}
    blk = lambda e: e ^ rank ^ 7
    for c in range(2):
        exps = sorted(e for e in range(N) if blk(e) // 4 == c)
        ks, k0 = [], []
        for b in range(4):
            q = "sv"[b % 2]
            o = 512 * (4 * c + b)
            if 0 in exps:
                p = B2 + CK * (b % 2)
                k0.append(cp(q, T["pp%d" % (b // 2)][:, p:p + CK], T.ps[:, o + CK * (blk(0) % 4):o + CK * (blk(0) % 4) + CK], k_d[(c, b)]))
            ks.append(cp(q, T.vv[:, 4 * c:4 * c + 4, CK * b:CK * b + CK], T.ps[:, o:o + HALF], k_d[(c, b)]))
        for e in exps:
            done[e] = [ks[0:2] + k0[0:2], ks[2:4] + k0[2:4]]
        while nxt[0] in done:
            e = nxt[0]
            for h in range(2):
                P = T["pp%d" % h]
                if e == 0:
                    k_p[(0, h)] = done[0][h]
                else:
                    k_p[(e, h)] = run("v", lambda: V.tensor_tensor(P[:, B2 * (e + 1):B2 * (e + 2)], P[:, 0:B2 * (e + 1)].indirect(T.po[:, 6 * e:6 * e + 6]),
                                                                   T.vv[:, blk(e), B2 * h:B2 * h + B2], A.add), k_p[(e - 1, h)], done[e][h], k_po, c_pp)
            nxt[0] += 1
    ny = 0
    for h in range(2):
        ks = []
        for b in (0, 2, 1, 3):
            ks.append(cp("sv"[b // 2], T.yo[:, 512 * h + b:512 * (h + 1):4], T["pp%d" % (b // 2)][:, :].indirect(T.lb[:, 16 * (b % 2) + 8 * h:16 * (b % 2) + 8 * h + 8]),
                         k_p[(7, b // 2)], k_lb[b % 2]))
        need("y", ks)
        g.sync.dma_start(T.y[:, 512 * h:512 * h + 512], T.yo[:, 512 * h:512 * h + 512]).then_inc(T.sem.dy, 16)
        ny += 16
    need("y", ("dy", ny))
    need("p", [("v", cnt["v"]), ("s", cnt["s"]), ("t", cnt["t"]), ("p", cnt["p"]), ("loc", loc[0])])
